import numpy as np
import ml_dtypes


def mxq(x, axis, fmt="e4m3"):
    dtype, down = {"e4m3": (ml_dtypes.float8_e4m3fn, 7), "e5m2": (ml_dtypes.float8_e5m2, 14)}[fmt]
    v = np.moveaxis(np.asarray(x, np.float32).astype(ml_dtypes.bfloat16).astype(np.float64), axis, -1)
    blocks = v.reshape(v.shape[:-1] + (-1, 32))
    amax = np.abs(blocks).max(-1, keepdims=True)
    byte = np.maximum(np.where(amax > 0, np.frexp(amax)[1] - 1 + 127, 0) - down, 1)
    scale = np.exp2(byte - 127.0)
    codes = (blocks / scale).astype(np.float32).astype(dtype).astype(np.float64)
    return np.moveaxis((codes * scale).reshape(v.shape), -1, axis)


WIDE = False


def mx_kscale(k):
    if not WIDE:
        return np.ones(k)
    levels = np.array([10, -10, 5, -5, 0])
    if k % 512:
        return np.exp2(np.random.permutation(np.resize(levels, k // 32))).repeat(32)
    a = np.empty((k // 512, 16))
    for p in range(k // 512):
        a[p, :8] = np.random.permutation(np.resize(levels, 8))
        for g in range(8):
            far = levels[np.abs(levels - a[p, g]) >= 10]
            a[p, g + 8] = far[np.random.randint(len(far))]
    return np.exp2(a.ravel()).repeat(32)


BF16 = ml_dtypes.bfloat16


def bf(x):
    return np.asarray(x, np.float32).astype(BF16)


def f64(x):
    return np.asarray(x).astype(np.float64)

def planes(Y):
    n, m = Y.shape
    b = f64(bf(Y)).reshape(n // 32, 32, m)
    amax = np.abs(b).max(1)
    byte = np.clip(np.where(amax > 0, np.frexp(amax)[1] - 1 + 127 - 7, 1), 1, 254)
    codes = (b * np.exp2(127.0 - byte)[:, None, :]).reshape(n, m).astype(np.float32).astype(ml_dtypes.float8_e4m3fn).view(np.uint8)
    words = codes.reshape(n // 512, 128, 4, m).transpose(0, 1, 3, 2)
    return np.ascontiguousarray(words), np.ascontiguousarray(byte.astype(np.uint8).reshape(n // 512, 16, m))


C, T, E, V = 2048, 1024, 1024, 512

def setup_inputs():
    r = np.random.randn
    dense = mx_kscale(E)
    lexical = mx_kscale(V)
    return {
        "query": bf(r(T, E)),
        "feedback": bf(r(T, E)),
        "w_query": bf(1.0 + 0.5 * r(E)),
        "w_feedback": bf(-1.0 + 0.5 * r(E)),
        "b_mix": bf(0.5 * r(E)),
        "gain": bf(np.exp(0.3 * r(E)) * dense),
        "docs": bf(1.5 * r(C, E) / np.sqrt(E) / dense),
        "query_terms": bf(r(T, V) / lexical),
        "doc_terms": bf(r(C, V) / np.sqrt(V) * lexical),
        "b_gate": bf(0.5 * r(T)),
        "prior": bf(np.exp(0.8 * r(C))),
    }

def reference(query, feedback, w_query, w_feedback, b_mix, gain, docs, query_terms, doc_terms, b_gate, prior):
    q, f = f64(query), f64(feedback)
    mix = 1.0 / (1.0 + np.exp(-(q * f64(w_query) + f * f64(w_feedback) + f64(b_mix))))
    rewritten = (mix * q + (1.0 - mix) * f) * f64(gain)
    score = mxq(f64(docs), 1, "e4m3") @ mxq(rewritten, 1, "e4m3").T
    match = mxq(f64(doc_terms), 1, "e4m3") @ mxq(f64(query_terms), 1, "e4m3").T
    gate = 1.0 / (1.0 + np.exp(-(match + f64(b_gate))))
    y = score * gate * f64(prior)[:, None]
    Y = y.reshape(C, T)
    words, scales = planes(Y)
    return y, words, scales

from contextlib import ExitStack

import concourse.mybir as mybir
from concourse.masks import make_identity

C, T, E, V = 2048, 1024, 1024, 512
FLOPS = 2 * C * T * (E + V)

F32 = mybir.dt.float32
BF16 = mybir.dt.bfloat16
U32 = mybir.dt.uint32
I32 = mybir.dt.int32
U8 = mybir.dt.uint8
FP8X4 = mybir.dt.float8_e4m3fn_x4
ALU = mybir.AluOpType
ACT = mybir.ActivationFunctionType

P = 128
PACK = 4
W = 512
HALF = W // 2

W_FEEDBACK, B_MIX, GAIN, W_QUERY, PRIOR, ROWS = 0, 2, 4, 6, 8, 12

BANKS, RAW_QUERIES, RAW_DOCS, RAW_TERMS, STAGES, GATES, OUT_CODES = 8, 4, 2, 3, 6, 6, 2

ORDER = """
Lf00 clear Lq00 Lw Tw warm F000 Ldt3 Z000 Lq01 Tdt3:v4 Lb D000 Qdt3 Sm000 F001 Lf01 Z001 Sm001 U000:g F010
Ldt0 D001 Tdt0:v0 Lqt1 Z010 Lqt0 Lf1 D010 U001:g Tqt0:s4 Lq1 Ld3 Ldt1 R000:v2 R001:v3 Sm010 Qr000 Qqt0 Tqt1:s1
F011 Qqt1 Ldt2 Z011 D011 Sm011 bias Qdt0 M300 M310 Qr001 F110 F111 Tdt2:s0 Z110 U010:g U011:g R011:g1 Z111
D110 Tdt1:s2 D111 M010 Sm110 R010:g3 Ld0 U110:g M000 Sm111 M001 M301 F100 Td31:s4 Z100 Sm100 D100 Qr010
Td30:s5 U111:g Qd31 Td00:s3 Qdt2 F101 U100:g Qdt1 Qd30 Td01:s4 Qd00 R111:g3 Ld2 Ld1 Qr011 M100 Sg300 M200 Z101
D101 M110 M311 Sm101 M201 Sg200 Qr111 Td10:s5 Qd10 S300 M101 Sg000 Sg201 Sg301 Td20:s3 S301 Td21:s1 C300:s5
Sg001 Qd20 Qd21 Qd01 U101:g Sg100 R101:g0 Qy300 R110:g4 Td11:s3 M111 S001 M011 S200 S000 S201 Qd11 Qr110
R100:g2 C301:s1 Qr100 Qr101 Sg101 Sg011 C001:g2 Qy301 Sg010 Sg111 Sg110 C000:s5 S100 C200:s0 S101 C201:s1 S110
S111 Sg311 Qy000 Qy200 Qy001 Sg310 C110:s5 C100:g3 S010 S011 M210 Qy201 Qy100 C101:s2 Qy101 Ss0 C111:g4 S311
C011:s0 S310 C010:s1 M211 Qy110 Qy010 Sg210 Qy111 Qy011 Sg211 S210 S211 C310:s3 C311:s5 Qy310 C211:v4 C210:s2
Qy311 Qy210 Qy211 Ss1
""".split()


def tile_query_rewrite_hybrid_score_g2_kernel(
    tc, query, feedback, w_query, w_feedback, b_mix, gain, docs, query_terms, doc_terms, b_gate, prior,
    out_0, out_1, out_2
):
    nc = tc.nc
    with ExitStack() as ctx:
        keep = ctx.enter_context(tc.tile_pool(name="keep", bufs=1))
        work = ctx.enter_context(tc.tile_pool(name="work", bufs=1))
        psum = ctx.enter_context(tc.psum_pool(name="psum", bufs=1))
        ctx.enter_context(tc.manual_schedule())

        ident = keep.tile([P, P], F32, align_bytes=64)
        warm = keep.tile([P, 1], F32)
        rows = keep.tile([P, W], BF16, align_bytes=64)
        consts = keep.tile([P, ROWS, PACK], F32)
        bias_col = keep.tile([P, 8], BF16)
        bias_row = keep.tile([P, T], BF16, align_bytes=64)
        doc_codes = keep.tile([P, 4, 2, W], U32, align_bytes=64)
        doc_scales = keep.tile([P, 4, 2, W], U8, align_bytes=64)
        dterm_codes = keep.tile([P, 4, W], U32, align_bytes=64)
        dterm_scales = keep.tile([P, 4, W], U8, align_bytes=64)
        rew_codes = keep.tile([P, 2, 2, W], U32, align_bytes=64)
        rew_scales = keep.tile([P, 2, 2, W], U8, align_bytes=64)
        qterm_codes = keep.tile([P, 2, W], U32, align_bytes=64)
        qterm_scales = keep.tile([P, 2, W], U8, align_bytes=64)
        y_scales = keep.tile([P, T], U8, align_bytes=64)

        tiles = {}
        taken = {}

        def turn(kind, count):
            n = taken.get(kind, 0)
            taken.update({kind: n + 1})
            return "%s%d" % (kind, n % count)

        def fresh(key, tag, shape, dtype):
            tile = work.tile(shape, dtype, name="_".join(str(x) for x in key), tag=tag, align_bytes=64)
            tiles.update({key: tile})
            return tile

        def bank():
            return psum.tile([P, W], F32, name="bank", tag=turn("bank", BANKS))

        def pairs(raw):
            return raw[:].rearrange("p a k -> p (a k)").bitcast(F32)

        def copy(engine, out, in_):
            if engine == "s":
                nc.scalar.copy(out=out, in_=in_)
            else:
                nc.vector.tensor_copy(out=out, in_=in_)

        def quantize(codes, scales, grouped):
            nc.vector.quantize_mx(out=codes.bitcast(FP8X4), scales=scales, in_=grouped[:])

        def interleaved(grouped):
            return grouped[:].rearrange("p (n i t) -> p n t i", i=2, t=PACK)

        def by_pairs(tile, h):
            return tile[:, :, HALF * h : HALF * (h + 1)].rearrange("p t (n i) -> p n t i", i=2)

        def clear():
            nc.vector.memset(rows[:], 0.0)
            make_identity(nc, ident[:])

        def warm_up():
            nc.scalar.activation(out=warm[:], in_=ident[:, 0:1], func=ACT.Sigmoid)

        def load_rows():
            for row, vector in ((W_FEEDBACK, w_feedback), (B_MIX, b_mix), (GAIN, gain), (W_QUERY, w_query), (PRIOR, prior)):
                count = vector.shape[0] // W
                nc.scalar.dma_start(out=rows[row : row + count, :], in_=vector.rearrange("(g k) -> g k", k=W))

        def turn_rows():
            acc = bank()
            words = rows[:].bitcast(F32)
            for u in range(2):
                nc.tensor.transpose(acc[:, u * P : (u + 1) * P], words[:, u:HALF:2], ident[:])
            turned = acc[:, 0:HALF].bitcast(BF16).rearrange("p (u r e) -> p u r e", u=2, e=2)
            nc.vector.tensor_copy(out=consts[:].rearrange("p r (u e) -> p u r e", u=2), in_=turned[:, :, 0:ROWS, :])

        def load_bias():
            nc.sync.dma_start(out=bias_col[:], in_=b_gate.rearrange("(n j) -> n j", n=P))

        def spread_bias():
            acc = bank()
            col = bias_col[:].bitcast(F32)
            for j in range(4):
                nc.tensor.transpose(acc[:, j * P : (j + 1) * P], col[:, j : j + 1].to_broadcast([P, P]), ident[:])
            nc.scalar.copy(out=bias_row[:].bitcast(F32).rearrange("p (n j) -> p n j", j=4),
                           in_=acc[:].rearrange("p (j n) -> p n j", j=4))

        def load_chunk(name, source, c, g):
            if not g:
                fresh((name, c), turn("raw_query", RAW_QUERIES), [P, 4, E], BF16)
            ks = slice(0, E) if g is None else slice(W * g, W * (g + 1))
            rows = source[W * c : W * (c + 1), :].rearrange("(a p) k -> p a k", p=P)
            nc.sync.dma_start(out=tiles[(name, c)][:, :, ks], in_=rows[:, :, ks])

        def load_query(c, g=None):
            load_chunk("query", query, c, g)

        def load_feedback(c, g=None):
            load_chunk("feedback", feedback, c, g)

        def load_qterms(c):
            raw = fresh(("qterms", c), turn("raw_terms", RAW_TERMS), [P, 4, V], BF16)
            nc.sync.dma_start(out=raw[:], in_=query_terms[W * c : W * (c + 1), :].rearrange("(a p) k -> p a k", p=P))

        def load_dterms(G):
            raw = fresh(("dterms", G), turn("raw_terms", RAW_TERMS), [P, PACK, V], BF16)
            nc.sync.dma_start(out=raw[:], in_=doc_terms[W * G : W * (G + 1), :].rearrange("(m t) k -> m t k", t=PACK))

        def load_docs(G):
            raw = fresh(("docs", G), turn("raw_docs", RAW_DOCS), [P, PACK, E], BF16)
            nc.sync.dma_start(out=raw[:], in_=docs[W * G : W * (G + 1), :].rearrange("(m t) k -> m t k", t=PACK))

        def turn_and_group(key, g, engine, slot):
            raw = tiles[key]
            words = pairs(raw)
            width = raw.shape[2] // 2
            grouped = fresh(key + ("grouped", g), "group%d" % slot, [P, W * PACK], BF16)
            for h in range(2):
                acc = bank()
                for j in range(2):
                    start = (2 * h + j) * width + HALF * g
                    for u in range(2):
                        col = (2 * j + u) * P
                        nc.tensor.transpose(acc[:, col : col + P], words[:, start + u : start + HALF : 2], ident[:])
                copy(engine,
                     grouped[:].bitcast(F32)[:, W * h : W * (h + 1)].rearrange("p (j m u) -> p j m u", j=2, u=2),
                     acc[:].rearrange("p (j u m) -> p j m u", j=2, u=2))

        def turn_qterms(c, engine, slot):
            turn_and_group(("qterms", c), 0, engine, slot)

        def turn_dterms(G, engine, slot):
            turn_and_group(("dterms", G), 0, engine, slot)

        def turn_docs(G, g, engine, slot):
            turn_and_group(("docs", G), g, engine, slot)

        def quant_qterms(c):
            quantize(qterm_codes[:, c, :], qterm_scales[:, c, :], tiles[("qterms", c, "grouped", 0)])

        def quant_dterms(G):
            quantize(dterm_codes[:, G, :], dterm_scales[:, G, :], tiles[("dterms", G, "grouped", 0)])

        def quant_docs(G, g):
            quantize(doc_codes[:, G, g, :], doc_scales[:, G, g, :], tiles[("docs", G, "grouped", g)])

        def turn_features(name, c, g, u):
            acc = bank()
            words = pairs(tiles[(name, c)])
            for a in range(4):
                start = a * (E // 2) + HALF * g
                nc.tensor.transpose(acc[:, a * P : (a + 1) * P], words[:, start + u : start + HALF : 2], ident[:])
            return acc[:].bitcast(BF16).rearrange("p (n e) -> p n e", e=2)

        def const(row, g, t):
            return consts[:, row + g, t : t + 1]

        def scale_feedback(c, g, u):
            turned = turn_features("feedback", c, g, u)
            if u == 0:
                fresh(("mix", c, g), turn("stage", STAGES), [P, PACK, W], F32)
                fresh(("base", c, g), turn("stage", STAGES), [P, PACK, W], F32)
            for e in range(2):
                t = 2 * u + e
                nc.scalar.activation(out=tiles[("mix", c, g)][:, t, :], in_=turned[:, :, e], func=ACT.Identity,
                                     scale=const(W_FEEDBACK, g, t), bias=const(B_MIX, g, t))
            for e in range(2):
                t = 2 * u + e
                nc.scalar.activation(out=tiles[("base", c, g)][:, t, :], in_=turned[:, :, e], func=ACT.Copy,
                                     scale=const(GAIN, g, t))

        def add_query(c, g, u):
            turned = turn_features("query", c, g, u)
            tiles.update({("turned_query", c, g, u): turned})
            for e in range(2):
                t = 2 * u + e
                mix = tiles[("mix", c, g)][:, t, :]
                nc.vector.scalar_tensor_tensor(out=mix, in0=turned[:, :, e], scalar=const(W_QUERY, g, t), in1=mix,
                                               op0=ALU.mult, op1=ALU.add)

        def difference(c, g, u):
            if u == 0:
                fresh(("diff", c, g), turn("stage", STAGES), [P, PACK, W], F32)
            for e in range(2):
                t = 2 * u + e
                nc.vector.scalar_tensor_tensor(out=tiles[("diff", c, g)][:, t, :], in0=tiles[("turned_query", c, g, u)][:, :, e],
                                               scalar=const(GAIN, g, t), in1=tiles[("base", c, g)][:, t, :],
                                               op0=ALU.mult, op1=ALU.subtract)

        def sigmoid(tile, h):
            part = tile[:, 2 * h : 2 * h + 2, :]
            nc.scalar.activation(out=part, in_=part, func=ACT.Sigmoid)

        def mix_sigmoid(c, g, u):
            sigmoid(tiles[("mix", c, g)], u)

        def weigh(c, g, u, engine):
            diff = tiles[("diff", c, g)][:, 2 * u : 2 * u + 2, :]
            (nc.gpsimd if engine == "g" else nc.vector).tensor_tensor(
                out=diff, in0=diff, in1=tiles[("mix", c, g)][:, 2 * u : 2 * u + 2, :], op=ALU.mult)

        def rewrite(c, g, h, engine, slot):
            grouped = fresh(("rewritten", c, g, h), "group%d" % slot, [P, HALF * PACK], BF16)
            (nc.gpsimd if engine == "g" else nc.vector).tensor_tensor(
                out=interleaved(grouped), in0=by_pairs(tiles[("diff", c, g)], h), in1=by_pairs(tiles[("base", c, g)], h), op=ALU.add)

        def quant_rewritten(c, g, h):
            cols = slice(HALF * h, HALF * (h + 1))
            quantize(rew_codes[:, c, g, cols], rew_scales[:, c, g, cols], tiles[("rewritten", c, g, h)])

        def match(G, c, h):
            if h == 0:
                n = taken.get("gate", 0)
                tag = turn("gate", GATES + 2)
                fresh(("y", G, c), tag if n < GATES else "raw_query%d" % (n - GATES), [P, PACK, W], F32)
            for t in (2 * h, 2 * h + 1):
                acc = bank()
                ms = slice(P * t, P * (t + 1))
                nc.tensor.matmul_mx(out=acc[:], lhsT=dterm_codes[:, G, ms].bitcast(FP8X4), lhsT_scale=dterm_scales[:, G, ms],
                                    rhs=qterm_codes[:, c, :].bitcast(FP8X4), rhs_scale=qterm_scales[:, c, :],
                                    start=True, stop=True)
                nc.vector.tensor_tensor(out=tiles[("y", G, c)][:, t, :], in0=acc[:], in1=bias_row[:, W * c : W * (c + 1)], op=ALU.add)

        def gate_sigmoid(G, c, h):
            sigmoid(tiles[("y", G, c)], h)

        def score(G, c, h):
            y = tiles[("y", G, c)]
            for t in (2 * h, 2 * h + 1):
                acc = bank()
                ms = slice(P * t, P * (t + 1))
                for g in range(2):
                    nc.tensor.matmul_mx(out=acc[:], lhsT=doc_codes[:, G, g, ms].bitcast(FP8X4), lhsT_scale=doc_scales[:, G, g, ms],
                                        rhs=rew_codes[:, c, g, :].bitcast(FP8X4), rhs_scale=rew_scales[:, c, g, :],
                                        start=(g == 0), stop=(g == 1))
                nc.vector.scalar_tensor_tensor(out=y[:, t, :], in0=acc[:], scalar=const(PRIOR, G, t), in1=y[:, t, :],
                                               op0=ALU.mult, op1=ALU.mult)
            rows = out_0[W * G : W * (G + 1), W * c : W * (c + 1)].rearrange("(m t) n -> m t n", t=PACK)
            nc.sync.dma_start(out=rows[:, 2 * h : 2 * h + 2, :], in_=y[:, 2 * h : 2 * h + 2, :])

        def cast(G, c, h, engine, slot):
            grouped = fresh(("y16", G, c, h), "group%d" % slot, [P, HALF * PACK], BF16)
            source = by_pairs(tiles[("y", G, c)], h)
            if engine == "g":
                nc.gpsimd.tensor_scalar(out=interleaved(grouped), in0=source, scalar1=1.0, scalar2=-0.0, op0=ALU.mult, op1=ALU.add)
            else:
                copy(engine, interleaved(grouped), source)

        def quant_y(G, c, h):
            if h == 0:
                fresh(("y_codes", G, c), turn("out_codes", OUT_CODES), [P, W], U32)
            codes = tiles[("y_codes", G, c)]
            first = W * c + HALF * h
            quantize(codes[:, HALF * h : HALF * (h + 1)], y_scales[4 * G : P, first : first + HALF], tiles[("y16", G, c, h)])
            if h == 1:
                words = out_1[G].rearrange("p n t -> p (n t)").bitcast(I32)
                nc.sync.dma_start(out=words[:, W * c : W * (c + 1)], in_=codes[:].bitcast(I32))

        def store_scales(c):
            cols = slice(W // 4 * c, W // 4 * (c + 1))
            for Q in range(4):
                nc.sync.dma_start(out=out_2.bitcast(I32)[:, 4 * Q : 4 * Q + 4, cols],
                                  in_=y_scales[:].bitcast(I32)[32 * Q : 32 * Q + 16, cols])

        steps = {
            "clear": clear, "warm": warm_up, "Lw": load_rows, "Tw": turn_rows,
            "Lb": load_bias, "bias": spread_bias, "Lq": load_query, "Lf": load_feedback, "Lqt": load_qterms,
            "Ldt": load_dterms, "Ld": load_docs, "Tqt": turn_qterms, "Tdt": turn_dterms, "Td": turn_docs,
            "Qqt": quant_qterms, "Qdt": quant_dterms, "Qd": quant_docs, "F": scale_feedback, "Z": add_query,
            "D": difference, "Sm": mix_sigmoid, "U": weigh, "R": rewrite, "Qr": quant_rewritten, "M": match,
            "Sg": gate_sigmoid, "S": score, "C": cast, "Qy": quant_y, "Ss": store_scales,
        }
        for step in ORDER:
            parts = step.split(":")
            name = "".join(ch for ch in parts[0] if ch not in "0123456789")
            indices = [int(ch) for ch in parts[0][len(name) :]]
            extra = [ch if ch in "svg" else int(ch) for ch in "".join(parts[1:])]
            steps[name](*indices, *extra)
